import numpy as np
import ml_dtypes


def mxq(x, axis, fmt="e4m3"):
    dtype, down = {"e4m3": (ml_dtypes.float8_e4m3fn, 7), "e5m2": (ml_dtypes.float8_e5m2, 14)}[fmt]
    v = np.moveaxis(np.asarray(x, np.float32).astype(ml_dtypes.bfloat16).astype(np.float64), axis, -1)
    blocks = v.reshape(v.shape[:-1] + (-1, 32))
    amax = np.abs(blocks).max(-1, keepdims=True)
    byte = np.maximum(np.where(amax > 0, np.frexp(amax)[1] - 1 + 127, 0) - down, 1)
    scale = np.exp2(byte - 127.0)
    codes = (blocks / scale).astype(np.float32).astype(dtype).astype(np.float64)
    return np.moveaxis((codes * scale).reshape(v.shape), -1, axis)


WIDE = False


def mx_kscale(k):
    if not WIDE:
        return np.ones(k)
    levels = np.array([10, -10, 5, -5, 0])
    if k % 512:
        return np.exp2(np.random.permutation(np.resize(levels, k // 32))).repeat(32)
    a = np.empty((k // 512, 16))
    for p in range(k // 512):
        a[p, :8] = np.random.permutation(np.resize(levels, 8))
        for g in range(8):
            far = levels[np.abs(levels - a[p, g]) >= 10]
            a[p, g + 8] = far[np.random.randint(len(far))]
    return np.exp2(a.ravel()).repeat(32)


def f64(x):
    return np.asarray(x).astype(np.float64)


def striped(idx):
    return np.tile(np.asarray(idx).reshape(-1, 16).T, (8, 1)).astype(np.uint16)


def unstriped(offs):
    return offs[:16].T.reshape(-1).astype(np.int64)


E2M1 = np.array([0.0, 0.5, 1.0, 1.5, 2.0, 3.0, 4.0, 6.0, -0.0, -0.5, -1.0, -1.5, -2.0, -3.0, -4.0, -6.0])


def pack_weight(w, fmt):
    k, n = w.shape
    w = f64(np.asarray(w, np.float32).astype(ml_dtypes.bfloat16)).reshape(k // 32, 32, n)
    amax = np.abs(w).max(1)
    if fmt == "e4m3":
        byte = np.frexp(amax)[1] - 1 + 127 - 7
    else:
        mant, ex = np.frexp(amax / 6.0)
        byte = np.where(mant > 0.5, ex, ex - 1) + 127
    byte = np.clip(np.where(amax > 0, byte, 1), 1, 254)
    scaled = (w * np.exp2(127.0 - byte)[:, None, :]).reshape(k, n).astype(np.float32)
    by_word = np.ascontiguousarray(scaled.reshape(k // 512, 128, 4, n).transpose(0, 1, 3, 2))
    if fmt == "e4m3":
        words = by_word.astype(ml_dtypes.float8_e4m3fn).view(np.uint8)
    else:
        c = by_word.astype(ml_dtypes.float4_e2m1fn).view(np.uint8) & 0xF
        words = (c[..., 0::2] | (c[..., 1::2] << 4)).reshape(k // 512, 128, 2 * n)
    return np.ascontiguousarray(words), np.ascontiguousarray(byte.astype(np.uint8).reshape(k // 512, 16, n))


def unpack_weight(words, scales, fmt):
    g, _, n = scales.shape
    words = np.ascontiguousarray(words).reshape(g, 128, n, -1)
    if fmt == "e4m3":
        vals = words.view(ml_dtypes.float8_e4m3fn).astype(np.float64)
    else:
        nib = np.empty((g, 128, n, 4), np.uint8)
        nib[..., 0::2] = words & 0xF
        nib[..., 1::2] = words >> 4
        vals = E2M1[nib]
    vals = vals * np.repeat(np.exp2(scales.astype(np.float64) - 127.0), 8, axis=1)[..., None]
    return vals.transpose(0, 1, 3, 2).reshape(g * 512, n)


B, N, T, D, DV, NQ = 1, 1024, 4096, 512, 256, 256
PAGE = 512


def setup_inputs():
    n = np.random.standard_normal
    pages = np.random.permutation(T // PAGE)[:B * N // PAGE]
    idx = (pages[:, None] * PAGE + np.arange(PAGE)[None, :]).reshape(-1)
    s = mx_kscale(D)[:, None]
    u = np.ones(T)
    u[idx] = mx_kscale(B * N)
    r = np.random.uniform(0.5, 2.0, T)
    k = n((D, T)) / s
    v = n((DV, T)) / (u * r)
    kp = pack_weight(k, "e4m3")
    vp = pack_weight(v.T, "e4m3")
    return {
        "qT": (n((B, D, NQ)) * s * (0.60 / np.sqrt(D))).astype(np.float32),
        "k_words": kp[0],
        "k_scales": kp[1],
        "v_words": vp[0],
        "v_scales": vp[1],
        "vs": np.tile(u * r, (128, 1)).astype(np.float32),
        "offs": striped(idx),
        "voffs": striped((pages[:, None] * DV + np.arange(DV)[None, :]).reshape(-1)),
    }


def reference(qT, k_words, k_scales, v_words, v_scales, vs, offs, voffs):
    idx = unstriped(offs)
    k = unpack_weight(k_words, k_scales, "e4m3")
    v = unpack_weight(v_words, v_scales, "e4m3")
    v = v.reshape(T // 512, 512, DV)[unstriped(voffs)[::DV] // DV].reshape(B, N, DV)
    pick = lambda x: x[:, idx].reshape(x.shape[0], B, N).transpose(1, 0, 2)
    q = f64(qT)
    score = mxq(q, 1, "e4m3").transpose(0, 2, 1) @ pick(k)
    p = np.square(np.maximum(score, 0.0))
    total = p.sum(-1, keepdims=True) + 1.0
    w = p * pick(f64(vs))[:, :1, :]
    y = mxq(w, 2, "e4m3") @ v
    y = y / total
    return y

@@ -1,0 +1,158 @@
+from contextlib import ExitStack
+
+import concourse.mybir as mybir
+from concourse.masks import make_identity
+
+F32 = mybir.dt.float32
+BF16 = mybir.dt.bfloat16
+I32 = mybir.dt.int32
+U32 = mybir.dt.uint32
+U16 = mybir.dt.uint16
+U8 = mybir.dt.uint8
+FP8X4 = mybir.dt.float8_e4m3fn_x4
+ACT = mybir.ActivationFunctionType
+ALU = mybir.AluOpType
+
+P = 128
+PACK = 4
+PAGE = P * PACK
+N, T, D, DV, NQ = 1024, 4096, 512, 256, 256
+PAGES = N // PAGE
+POOL_PAGES = T // PAGE
+Q_TILES = NQ // P
+LIST_ROWS = 16
+QUADRANT = 32
+PARK = 8
+VS_ROW = 4
+
+FLOPS = 2 * NQ * N * (D + DV)
+
+
+def place_scale_rows(nc, plane, parked):
+    nc.vector.tensor_copy(plane[:].bitcast(I32), parked[:].bitcast(I32))
+    for j in range(1, PACK):
+        nc.sync.dma_start(plane[j:P:QUADRANT, :].bitcast(I32), parked[PARK * j : P : QUADRANT, :].bitcast(I32))
+
+
+def tile_attend_pkv8_relu2_kernel(tc, qT, k_words, k_scales, v_words, v_scales, vs, offs, voffs, out):
+    nc = tc.nc
+    with ExitStack() as ctx:
+        lists = ctx.enter_context(tc.tile_pool(name="lists", bufs=1))
+        sb = ctx.enter_context(tc.tile_pool(name="sb", bufs=1))
+        psum = ctx.enter_context(tc.psum_pool(name="psum", bufs=1))
+
+        k_list = lists.tile([P, N // LIST_ROWS], U16, name="k_list")
+        v_list = lists.tile([P, PAGES * DV // LIST_ROWS], U16, name="v_list")
+        nc.sync.dma_start(k_list[:], offs)
+        nc.sync.dma_start(v_list[:], voffs)
+
+        q_raw = sb.tile([P, PACK, NQ], F32, name="q_raw")
+        nc.sync.dma_start(q_raw[:], qT[0].rearrange("(p j) c -> p j c", j=PACK))
+        k_pool = sb.tile([P, T], U32, name="k_pool", tag="k_then_v", align_bytes=64)
+        nc.sync.dma_start(k_pool[:].bitcast(I32), k_words[0].rearrange("p t r -> p (t r)").bitcast(I32))
+
+        ks_pool = sb.tile([P, T], U8, name="ks_pool", tag="ks_then_v", align_bytes=64)
+        nc.vector.memset(ks_pool[:].bitcast(I32), 0)
+        nc.scalar.dma_start(ks_pool[0:P:PARK, :].bitcast(I32), k_scales[0].bitcast(I32))
+        vsc_pool = sb.tile([P, POOL_PAGES * DV], U8, name="vsc_pool")
+        nc.vector.memset(vsc_pool[:].bitcast(I32), 0)
+        nc.scalar.dma_start(
+            vsc_pool[0:P:PARK, :].bitcast(I32).rearrange("f (u e) -> f u e", u=POOL_PAGES),
+            v_scales.bitcast(I32).rearrange("u f e -> f u e"),
+        )
+        ts_pool = sb.tile([P, T], F32, name="ts_pool", tag="ts_then_k", align_bytes=64)
+        nc.vector.memset(ts_pool[:], 0.0)
+        nc.scalar.dma_start(ts_pool[VS_ROW : VS_ROW + 1, :], vs[0:1, :])
+
+        ident = sb.tile([P, P], F32, name="ident")
+        make_identity(nc, ident[:])
+
+        ks_parked = sb.tile([P, N], U8, name="ks_parked")
+        nc.vector.tensor_copy(ks_parked[:], ks_pool[:].indirect(k_list[:]))
+        ks_plane = sb.tile([P, N], U8, name="ks_plane", align_bytes=64)
+        place_scale_rows(nc, ks_plane, ks_parked)
+
+        v_pool = sb.tile([P, POOL_PAGES * DV], U32, name="v_pool", tag="ks_then_v", align_bytes=64)
+        nc.sync.dma_start(
+            v_pool[:].bitcast(I32).rearrange("p (u e) -> p u e", u=POOL_PAGES),
+            v_words.rearrange("u p e r -> p u (e r)").bitcast(I32),
+        )
+
+        q_bf = sb.tile([P, NQ, PACK], BF16, name="q_bf", align_bytes=64)
+        nc.scalar.activation(q_bf[:], q_raw[:].rearrange("p j c -> p c j"), ACT.Copy)
+        q_codes = sb.tile([P, NQ], U32, name="q_codes", align_bytes=64)
+        q_plane = sb.tile([P, NQ], U8, name="q_plane", align_bytes=64)
+        nc.vector.quantize_mx(q_codes[:].bitcast(FP8X4), q_plane[:], q_bf[:].rearrange("p c j -> p (c j)"))
+
+        vsc_parked = sb.tile([P, PAGES * DV], U8, name="vsc_parked")
+        nc.vector.tensor_copy(vsc_parked[:], vsc_pool[:].indirect(v_list[:]))
+        vsc_plane = sb.tile([P, PAGES * DV], U8, name="vsc_plane", align_bytes=64)
+        place_scale_rows(nc, vsc_plane, vsc_parked)
+
+        ts_row = sb.tile([P, N], F32, name="ts_row")
+        cols = PAGE // LIST_ROWS
+        ts_col = sb.tile([P, PAGES, PACK], F32, name="ts_col")
+        for u in range(PAGES):
+            nc.vector.tensor_copy(ts_row[:, u * PAGE : (u + 1) * PAGE], ts_pool[:].indirect(k_list[:, u * cols : (u + 1) * cols]))
+            turned = psum.tile([P, PACK, P], F32, name="turned", tag="turned", bufs=3)
+            for r in range(PACK):
+                nc.tensor.transpose(turned[:, r, :], ts_row[:, u * PAGE + r : (u + 1) * PAGE : PACK], ident[:])
+            nc.scalar.copy(ts_col[:, u, :], turned[:, :, VS_ROW])
+
+        k_pages = sb.tile([P, N], U32, name="k_pages", tag="ts_then_k", align_bytes=64)
+        for u in range(PAGES):
+            nc.vector.tensor_copy(k_pages[:, u * PAGE : (u + 1) * PAGE], k_pool[:].indirect(k_list[:, u * cols : (u + 1) * cols]))
+        v_pages = sb.tile([P, PAGES * DV], U32, name="v_pages", tag="k_then_v", align_bytes=64)
+        nc.vector.tensor_copy(v_pages[:], v_pool[:].indirect(v_list[:]))
+
+        part_sum = sb.tile([P, Q_TILES, PAGES], F32, name="part_sum")
+        for h in range(Q_TILES):
+            rows = slice(h * P, (h + 1) * P)
+            acc = psum.tile([P, DV], F32, name=f"acc{h}")
+            for u in range(PAGES):
+                score = psum.tile([P, PAGE], F32, name="score", tag="score", bufs=3)
+                nc.tensor.matmul_mx(
+                    score[:],
+                    lhsT=q_codes[:, rows].bitcast(FP8X4),
+                    lhsT_scale=q_plane[:, rows],
+                    rhs=k_pages[:, u * PAGE : (u + 1) * PAGE].bitcast(FP8X4),
+                    rhs_scale=ks_plane[:, u * PAGE : (u + 1) * PAGE],
+                    start=True,
+                    stop=True,
+                )
+                pos = sb.tile([P, PACK, P], F32, name=f"pos{h}{u}")
+                if (h, u) in []:
+                    nc.vector.tensor_scalar(pos[:], score[:].rearrange("q (s r) -> q r s", r=PACK), 0.0, None, ALU.max)
+                else:
+                    nc.scalar.activation(pos[:], score[:].rearrange("q (s r) -> q r s", r=PACK), ACT.Relu)
+                p = sb.tile([P, PACK, P], F32, name=f"p{h}{u}")
+                nc.scalar.activation(p[:], pos[:], ACT.Square, accum_out=part_sum[:, h, u : u + 1])
+                turned = psum.tile([P, PACK, P], F32, name="turned", tag="turned", bufs=3)
+                for r in range(PACK):
+                    nc.tensor.transpose(turned[:, r, :], p[:, r, :], ident[:])
+                w = sb.tile([P, P, PACK], BF16, name=f"w{h}{u}", align_bytes=64)
+                nc.vector.tensor_tensor(
+                    w[:],
+                    turned[:].rearrange("s r q -> s q r"),
+                    ts_col[:, u, :].unsqueeze(1).to_broadcast([P, P, PACK]),
+                    ALU.mult,
+                )
+                w_codes = sb.tile([P, P], U32, name=f"w_codes{h}{u}", align_bytes=64)
+                w_plane = sb.tile([P, P], U8, name=f"w_plane{h}{u}", align_bytes=64)
+                nc.vector.quantize_mx(w_codes[:].bitcast(FP8X4), w_plane[:], w[:].rearrange("s q r -> s (q r)"))
+                nc.tensor.matmul_mx(
+                    acc[:],
+                    lhsT=w_codes[:].bitcast(FP8X4),
+                    lhsT_scale=w_plane[:],
+                    rhs=v_pages[:, u * DV : (u + 1) * DV].bitcast(FP8X4),
+                    rhs_scale=vsc_plane[:, u * DV : (u + 1) * DV],
+                    start=(u == 0),
+                    stop=(u == PAGES - 1),
+                )
+            total = sb.tile([P, 1], F32, name=f"total{h}")
+            nc.vector.tensor_scalar(total[:], part_sum[:, h, 0:1], part_sum[:, h, 1:2], 1.0, ALU.add, ALU.add)
+            inv = sb.tile([P, 1], F32, name=f"inv{h}")
+            nc.vector.reciprocal(inv[:], total[:])
+            y = sb.tile([P, DV], F32, name=f"y{h}")
+            nc.scalar.activation(y[:], acc[:], ACT.Copy, scale=inv[:])
+            nc.sync.dma_start(out[0, rows, :], y[:])

@@ -21,17 +21,23 @@ PAGES = N // PAGE
 POOL_PAGES = T // PAGE
 Q_TILES = NQ // P
 LIST_ROWS = 16
+SCALE_ROWS = 16
 QUADRANT = 32
-PARK = 8
+PARK_FIRST = 32
+PARK_STEP = 4
+PARKED = slice(PARK_FIRST, PARK_FIRST + SCALE_ROWS * PARK_STEP, PARK_STEP)
 VS_ROW = 4
 
 FLOPS = 2 * NQ * N * (D + DV)
 
 
 def place_scale_rows(nc, plane, parked):
-    nc.vector.tensor_copy(plane[:].bitcast(I32), parked[:].bitcast(I32))
-    for j in range(1, PACK):
-        nc.sync.dma_start(plane[j:P:QUADRANT, :].bitcast(I32), parked[PARK * j : P : QUADRANT, :].bitcast(I32))
+    for quad in range(P // QUADRANT):
+        first = PARK_FIRST + quad * PACK * PARK_STEP
+        nc.sync.dma_start(
+            plane[quad * QUADRANT : quad * QUADRANT + PACK, :].bitcast(I32),
+            parked[first : first + PACK * PARK_STEP : PARK_STEP, :].bitcast(I32),
+        )
 
 
 def tile_attend_pkv8_relu2_kernel(tc, qT, k_words, k_scales, v_words, v_scales, vs, offs, voffs, out):
@@ -43,33 +49,40 @@ def tile_attend_pkv8_relu2_kernel(tc, qT, k_words, k_scales, v_words, v_scales, 
 
         k_list = lists.tile([P, N // LIST_ROWS], U16, name="k_list")
         v_list = lists.tile([P, PAGES * DV // LIST_ROWS], U16, name="v_list")
-        nc.sync.dma_start(k_list[:], offs)
-        nc.sync.dma_start(v_list[:], voffs)
-
-        q_raw = sb.tile([P, PACK, NQ], F32, name="q_raw")
-        nc.sync.dma_start(q_raw[:], qT[0].rearrange("(p j) c -> p j c", j=PACK))
-        k_pool = sb.tile([P, T], U32, name="k_pool", tag="k_then_v", align_bytes=64)
-        nc.sync.dma_start(k_pool[:].bitcast(I32), k_words[0].rearrange("p t r -> p (t r)").bitcast(I32))
-
-        ks_pool = sb.tile([P, T], U8, name="ks_pool", tag="ks_then_v", align_bytes=64)
-        nc.vector.memset(ks_pool[:].bitcast(I32), 0)
-        nc.scalar.dma_start(ks_pool[0:P:PARK, :].bitcast(I32), k_scales[0].bitcast(I32))
+        q_raw = sb.tile([P, PACK, NQ], F32, name="q_raw", tag="q_then_plane", align_bytes=64)
         vsc_pool = sb.tile([P, POOL_PAGES * DV], U8, name="vsc_pool")
-        nc.vector.memset(vsc_pool[:].bitcast(I32), 0)
-        nc.scalar.dma_start(
-            vsc_pool[0:P:PARK, :].bitcast(I32).rearrange("f (u e) -> f u e", u=POOL_PAGES),
-            v_scales.bitcast(I32).rearrange("u f e -> f u e"),
-        )
-        ts_pool = sb.tile([P, T], F32, name="ts_pool", tag="ts_then_k", align_bytes=64)
-        nc.vector.memset(ts_pool[:], 0.0)
-        nc.scalar.dma_start(ts_pool[VS_ROW : VS_ROW + 1, :], vs[0:1, :])
-
+        ks_pool = sb.tile([P, T], U8, name="ks_pool", tag="ks_then_v", align_bytes=64)
+        k_pool = sb.tile([P, T], U32, name="k_pool", tag="k_then_ts", align_bytes=64)
+        ts_pool = sb.tile([P, T], F32, name="ts_pool")
+        ks_plane = sb.tile([P, N], U8, name="ks_plane", align_bytes=64)
         ident = sb.tile([P, P], F32, name="ident")
+
+        nc.gpsimd.memset(vsc_pool[:].bitcast(I32), 0)
+        nc.vector.memset(ks_pool[:].bitcast(I32)[:, :511], 0)
+        nc.vector.memset(ks_pool[:].bitcast(I32)[:, 511:], 0)
+        nc.gpsimd.memset(ts_pool[:, 1536:], 0.0)
+        nc.vector.memset(ts_pool[:, :767], 0.0)
+        nc.vector.memset(ts_pool[:, 767:1536], 0.0)
+        nc.gpsimd.memset(ks_plane[:].bitcast(I32), 0)
         make_identity(nc, ident[:])
 
+        k_dram = k_words[0].rearrange("p t r -> p (t r)").bitcast(I32)
+        nc.sync.dma_start(v_list[:], voffs)
+        nc.sync.dma_start(
+            vsc_pool[PARKED, :].bitcast(I32).rearrange("f (u e) -> f u e", u=POOL_PAGES),
+            v_scales.bitcast(I32).rearrange("u f e -> f u e"),
+        )
+        nc.sync.dma_start(k_list[:], offs)
+        nc.sync.dma_start(q_raw[:], qT[0].rearrange("(p j) c -> p j c", j=PACK))
+        nc.sync.dma_start(ks_pool[PARKED, :].bitcast(I32), k_scales[0].bitcast(I32))
+        nc.sync.dma_start(k_pool[:, : T // 2].bitcast(I32), k_dram[:, : T // 2])
+        nc.sync.dma_start(ts_pool[VS_ROW : VS_ROW + 1, :], vs[0:1, :])
+        nc.sync.dma_start(k_pool[:, T // 2 :].bitcast(I32), k_dram[:, T // 2 :])
+
+        vsc_parked = sb.tile([P, PAGES * DV], U8, name="vsc_parked")
+        nc.vector.tensor_copy(vsc_parked[:], vsc_pool[:].indirect(v_list[:]))
         ks_parked = sb.tile([P, N], U8, name="ks_parked")
         nc.vector.tensor_copy(ks_parked[:], ks_pool[:].indirect(k_list[:]))
-        ks_plane = sb.tile([P, N], U8, name="ks_plane", align_bytes=64)
         place_scale_rows(nc, ks_plane, ks_parked)
 
         v_pool = sb.tile([P, POOL_PAGES * DV], U32, name="v_pool", tag="ks_then_v", align_bytes=64)
@@ -84,75 +97,92 @@ def tile_attend_pkv8_relu2_kernel(tc, qT, k_words, k_scales, v_words, v_scales, 
         q_plane = sb.tile([P, NQ], U8, name="q_plane", align_bytes=64)
         nc.vector.quantize_mx(q_codes[:].bitcast(FP8X4), q_plane[:], q_bf[:].rearrange("p c j -> p (c j)"))
 
-        vsc_parked = sb.tile([P, PAGES * DV], U8, name="vsc_parked")
-        nc.vector.tensor_copy(vsc_parked[:], vsc_pool[:].indirect(v_list[:]))
-        vsc_plane = sb.tile([P, PAGES * DV], U8, name="vsc_plane", align_bytes=64)
+        vsc_plane = sb.tile([P, PAGES * DV], U8, name="vsc_plane", tag="q_then_plane", align_bytes=64)
+        nc.gpsimd.memset(vsc_plane[:].bitcast(I32), 0)
         place_scale_rows(nc, vsc_plane, vsc_parked)
 
-        ts_row = sb.tile([P, N], F32, name="ts_row")
         cols = PAGE // LIST_ROWS
-        ts_col = sb.tile([P, PAGES, PACK], F32, name="ts_col")
-        for u in range(PAGES):
-            nc.vector.tensor_copy(ts_row[:, u * PAGE : (u + 1) * PAGE], ts_pool[:].indirect(k_list[:, u * cols : (u + 1) * cols]))
-            turned = psum.tile([P, PACK, P], F32, name="turned", tag="turned", bufs=3)
-            for r in range(PACK):
-                nc.tensor.transpose(turned[:, r, :], ts_row[:, u * PAGE + r : (u + 1) * PAGE : PACK], ident[:])
-            nc.scalar.copy(ts_col[:, u, :], turned[:, :, VS_ROW])
+        ts_cols = [sb.tile([P, PACK], F32, name=f"ts_col{u}") for u in range(PAGES)]
 
-        k_pages = sb.tile([P, N], U32, name="k_pages", tag="ts_then_k", align_bytes=64)
+        def gather_token_scales(u, ts_row):
+            nc.vector.tensor_copy(ts_row[:], ts_pool[:].indirect(k_list[:, u * cols : (u + 1) * cols]))
+
+        def turn_token_scales(u, ts_row, bank_tag, copy):
+            bank = psum.tile([P, PACK, P], F32, name=f"ts_bank{u}", tag=bank_tag)
+            for r in range(PACK):
+                nc.tensor.transpose(bank[:, r, :], ts_row[:, r:PAGE:PACK], ident[:])
+            copy(ts_cols[u][:], bank[:, :, VS_ROW])
+
+        ts_row0 = sb.tile([P, PAGE], F32, name="ts_row0")
+        gather_token_scales(0, ts_row0)
+        turn_token_scales(0, ts_row0, "turn2", nc.scalar.copy)
+        ts_row1 = sb.tile([P, PAGE], F32, name="ts_row1")
+        gather_token_scales(1, ts_row1)
+        turn_token_scales(1, ts_row1, "turn1", nc.scalar.copy)
+        k_pages = []
         for u in range(PAGES):
-            nc.vector.tensor_copy(k_pages[:, u * PAGE : (u + 1) * PAGE], k_pool[:].indirect(k_list[:, u * cols : (u + 1) * cols]))
-        v_pages = sb.tile([P, PAGES * DV], U32, name="v_pages", tag="k_then_v", align_bytes=64)
+            k_page = sb.tile([P, PAGE], U32, name=f"k_page{u}", align_bytes=64)
+            nc.vector.tensor_copy(k_page[:], k_pool[:].indirect(k_list[:, u * cols : (u + 1) * cols]))
+            k_pages.append(k_page)
+        v_pages = sb.tile([P, PAGES * DV], U32, name="v_pages", align_bytes=64)
         nc.vector.tensor_copy(v_pages[:], v_pool[:].indirect(v_list[:]))
 
-        part_sum = sb.tile([P, Q_TILES, PAGES], F32, name="part_sum")
-        for h in range(Q_TILES):
-            rows = slice(h * P, (h + 1) * P)
-            acc = psum.tile([P, DV], F32, name=f"acc{h}")
-            for u in range(PAGES):
-                score = psum.tile([P, PAGE], F32, name="score", tag="score", bufs=3)
+        part_sum = sb.tile([P, PAGES, Q_TILES], F32, name="part_sum")
+        acc = [psum.tile([P, DV], F32, name=f"acc{h}") for h in range(Q_TILES)]
+        for u in range(PAGES):
+            w = sb.tile([P, Q_TILES, P, PACK], BF16, name=f"w{u}", align_bytes=64)
+            w_codes = sb.tile([P, NQ], U32, name=f"w_codes{u}", align_bytes=64)
+            w_plane = sb.tile([P, NQ], U8, name=f"w_plane{u}", align_bytes=64)
+            joint = u in [0]
+            for h in range(Q_TILES):
+                rows = slice(h * P, (h + 1) * P)
+                unit = u * Q_TILES + h
+                score = psum.tile([P, PAGE], F32, name=f"score{unit}", tag=f"score{unit % 3}")
                 nc.tensor.matmul_mx(
                     score[:],
                     lhsT=q_codes[:, rows].bitcast(FP8X4),
                     lhsT_scale=q_plane[:, rows],
-                    rhs=k_pages[:, u * PAGE : (u + 1) * PAGE].bitcast(FP8X4),
+                    rhs=k_pages[u][:].bitcast(FP8X4),
                     rhs_scale=ks_plane[:, u * PAGE : (u + 1) * PAGE],
                     start=True,
                     stop=True,
                 )
-                pos = sb.tile([P, PACK, P], F32, name=f"pos{h}{u}")
-                if (h, u) in []:
+                pos = sb.tile([P, PACK, P], F32, name=f"pos{unit}")
+                if unit in [3]:
                     nc.vector.tensor_scalar(pos[:], score[:].rearrange("q (s r) -> q r s", r=PACK), 0.0, None, ALU.max)
                 else:
                     nc.scalar.activation(pos[:], score[:].rearrange("q (s r) -> q r s", r=PACK), ACT.Relu)
-                p = sb.tile([P, PACK, P], F32, name=f"p{h}{u}")
-                nc.scalar.activation(p[:], pos[:], ACT.Square, accum_out=part_sum[:, h, u : u + 1])
-                turned = psum.tile([P, PACK, P], F32, name="turned", tag="turned", bufs=3)
+                p = sb.tile([P, PACK, P], F32, name=f"p{unit}")
+                nc.scalar.activation(p[:], pos[:], ACT.Square, accum_out=part_sum[:, u, h : h + 1])
+                turned = psum.tile([P, PACK, P], F32, name=f"turned{unit}", tag=f"turn{unit % 3}")
                 for r in range(PACK):
                     nc.tensor.transpose(turned[:, r, :], p[:, r, :], ident[:])
-                w = sb.tile([P, P, PACK], BF16, name=f"w{h}{u}", align_bytes=64)
                 nc.vector.tensor_tensor(
-                    w[:],
+                    w[:, h, :, :],
                     turned[:].rearrange("s r q -> s q r"),
-                    ts_col[:, u, :].unsqueeze(1).to_broadcast([P, P, PACK]),
+                    ts_cols[u][:].unsqueeze(1).to_broadcast([P, P, PACK]),
                     ALU.mult,
                 )
-                w_codes = sb.tile([P, P], U32, name=f"w_codes{h}{u}", align_bytes=64)
-                w_plane = sb.tile([P, P], U8, name=f"w_plane{h}{u}", align_bytes=64)
-                nc.vector.quantize_mx(w_codes[:].bitcast(FP8X4), w_plane[:], w[:].rearrange("s q r -> s (q r)"))
+                if not joint:
+                    nc.vector.quantize_mx(w_codes[:, rows].bitcast(FP8X4), w_plane[:, rows], w[:, h, :, :].rearrange("s q r -> s (q r)"))
+            if joint:
+                nc.vector.quantize_mx(w_codes[:].bitcast(FP8X4), w_plane[:], w[:].rearrange("s h q r -> s (h q r)"))
+            for h in range(Q_TILES):
+                rows = slice(h * P, (h + 1) * P)
                 nc.tensor.matmul_mx(
-                    acc[:],
-                    lhsT=w_codes[:].bitcast(FP8X4),
-                    lhsT_scale=w_plane[:],
+                    acc[h][:],
+                    lhsT=w_codes[:, rows].bitcast(FP8X4),
+                    lhsT_scale=w_plane[:, rows],
                     rhs=v_pages[:, u * DV : (u + 1) * DV].bitcast(FP8X4),
                     rhs_scale=vsc_plane[:, u * DV : (u + 1) * DV],
                     start=(u == 0),
                     stop=(u == PAGES - 1),
                 )
-            total = sb.tile([P, 1], F32, name=f"total{h}")
-            nc.vector.tensor_scalar(total[:], part_sum[:, h, 0:1], part_sum[:, h, 1:2], 1.0, ALU.add, ALU.add)
-            inv = sb.tile([P, 1], F32, name=f"inv{h}")
-            nc.vector.reciprocal(inv[:], total[:])
+        total = sb.tile([P, Q_TILES], F32, name="total")
+        nc.vector.scalar_tensor_tensor(total[:], part_sum[:, 0, :], 1.0, part_sum[:, 1, :], ALU.add, ALU.add)
+        inv = sb.tile([P, Q_TILES], F32, name="inv")
+        nc.vector.reciprocal(inv[:], total[:])
+        for h in range(Q_TILES):
             y = sb.tile([P, DV], F32, name=f"y{h}")
-            nc.scalar.activation(y[:], acc[:], ACT.Copy, scale=inv[:])
-            nc.sync.dma_start(out[0, rows, :], y[:])
+            nc.scalar.activation(y[:], acc[h][:], ACT.Copy, scale=inv[:, h : h + 1])
+            nc.scalar.dma_start(out[0, h * P : (h + 1) * P, :], y[:])

@@ -49,38 +49,34 @@ def tile_attend_pkv8_relu2_kernel(tc, qT, k_words, k_scales, v_words, v_scales, 
 
         k_list = lists.tile([P, N // LIST_ROWS], U16, name="k_list")
         v_list = lists.tile([P, PAGES * DV // LIST_ROWS], U16, name="v_list")
-        q_raw = sb.tile([P, PACK, NQ], F32, name="q_raw", tag="q_then_plane", align_bytes=64)
+        q_raw = sb.tile([P, PACK, NQ], F32, name="q_raw", align_bytes=64)
         vsc_pool = sb.tile([P, POOL_PAGES * DV], U8, name="vsc_pool")
         ks_pool = sb.tile([P, T], U8, name="ks_pool", tag="ks_then_v", align_bytes=64)
-        k_pool = sb.tile([P, T], U32, name="k_pool", tag="k_then_ts", align_bytes=64)
-        ts_pool = sb.tile([P, T], F32, name="ts_pool")
+        k_pool = sb.tile([P, T], U32, name="k_pool")
+        ts_pool = sb.tile([P, T], F32, name="ts_pool", tag="ts_then_vsc")
         ks_plane = sb.tile([P, N], U8, name="ks_plane", align_bytes=64)
         ident = sb.tile([P, P], F32, name="ident")
 
-        nc.gpsimd.memset(vsc_pool[:].bitcast(I32), 0)
-        nc.vector.memset(ks_pool[:].bitcast(I32)[:, :511], 0)
-        nc.vector.memset(ks_pool[:].bitcast(I32)[:, 511:], 0)
-        nc.gpsimd.memset(ts_pool[:, 1536:], 0.0)
-        nc.vector.memset(ts_pool[:, :767], 0.0)
-        nc.vector.memset(ts_pool[:, 767:1536], 0.0)
-        nc.gpsimd.memset(ks_plane[:].bitcast(I32), 0)
-        make_identity(nc, ident[:])
+        vsc_plane = sb.tile([P, PAGES * DV], U8, name="vsc_plane", align_bytes=64)
+        nc.vector.memset(ks_pool[:].bitcast(I32), 0)
+        nc.vector.memset(ts_pool[:], 0.0)
+        nc.vector.memset(vsc_pool[:].bitcast(I32), 0)
+        nc.vector.memset(ident[:], 0.0)
+        make_identity(nc, ident[:], nomemset=True)
 
         k_dram = k_words[0].rearrange("p t r -> p (t r)").bitcast(I32)
-        nc.sync.dma_start(v_list[:], voffs)
-        nc.sync.dma_start(
-            vsc_pool[PARKED, :].bitcast(I32).rearrange("f (u e) -> f u e", u=POOL_PAGES),
-            v_scales.bitcast(I32).rearrange("u f e -> f u e"),
-        )
         nc.sync.dma_start(k_list[:], offs)
+        nc.sync.dma_start(v_list[:], voffs)
         nc.sync.dma_start(q_raw[:], qT[0].rearrange("(p j) c -> p j c", j=PACK))
         nc.sync.dma_start(ks_pool[PARKED, :].bitcast(I32), k_scales[0].bitcast(I32))
         nc.sync.dma_start(k_pool[:, : T // 2].bitcast(I32), k_dram[:, : T // 2])
         nc.sync.dma_start(ts_pool[VS_ROW : VS_ROW + 1, :], vs[0:1, :])
+        nc.sync.dma_start(
+            vsc_pool[PARKED, :].bitcast(I32).rearrange("f (u e) -> f u e", u=POOL_PAGES),
+            v_scales.bitcast(I32).rearrange("u f e -> f u e"),
+        )
         nc.sync.dma_start(k_pool[:, T // 2 :].bitcast(I32), k_dram[:, T // 2 :])
 
-        vsc_parked = sb.tile([P, PAGES * DV], U8, name="vsc_parked")
-        nc.vector.tensor_copy(vsc_parked[:], vsc_pool[:].indirect(v_list[:]))
         ks_parked = sb.tile([P, N], U8, name="ks_parked")
         nc.vector.tensor_copy(ks_parked[:], ks_pool[:].indirect(k_list[:]))
         place_scale_rows(nc, ks_plane, ks_parked)
@@ -97,9 +93,6 @@ def tile_attend_pkv8_relu2_kernel(tc, qT, k_words, k_scales, v_words, v_scales, 
         q_plane = sb.tile([P, NQ], U8, name="q_plane", align_bytes=64)
         nc.vector.quantize_mx(q_codes[:].bitcast(FP8X4), q_plane[:], q_bf[:].rearrange("p c j -> p (c j)"))
 
-        vsc_plane = sb.tile([P, PAGES * DV], U8, name="vsc_plane", tag="q_then_plane", align_bytes=64)
-        nc.gpsimd.memset(vsc_plane[:].bitcast(I32), 0)
-        place_scale_rows(nc, vsc_plane, vsc_parked)
 
         cols = PAGE // LIST_ROWS
         ts_cols = [sb.tile([P, PACK], F32, name=f"ts_col{u}") for u in range(PAGES)]
@@ -119,6 +112,10 @@ def tile_attend_pkv8_relu2_kernel(tc, qT, k_words, k_scales, v_words, v_scales, 
         ts_row1 = sb.tile([P, PAGE], F32, name="ts_row1")
         gather_token_scales(1, ts_row1)
         turn_token_scales(1, ts_row1, "turn1", nc.scalar.copy)
+        vsc_parked = sb.tile([P, PAGES * DV], U8, name="vsc_parked", tag="ts_then_vsc")
+        nc.vector.tensor_copy(vsc_parked[:], vsc_pool[:].indirect(v_list[:]))
+        place_scale_rows(nc, vsc_plane, vsc_parked)
+
         k_pages = []
         for u in range(PAGES):
             k_page = sb.tile([P, PAGE], U32, name=f"k_page{u}", align_bytes=64)

from contextlib import ExitStack

import concourse.mybir as mybir
from concourse.masks import make_identity

F32 = mybir.dt.float32
BF16 = mybir.dt.bfloat16
I32 = mybir.dt.int32
U32 = mybir.dt.uint32
U16 = mybir.dt.uint16
U8 = mybir.dt.uint8
FP8X4 = mybir.dt.float8_e4m3fn_x4
ACT = mybir.ActivationFunctionType
ALU = mybir.AluOpType

P = 128
PACK = 4
PAGE = P * PACK
N, T, D, DV, NQ = 1024, 4096, 512, 256, 256
PAGES = N // PAGE
POOL_PAGES = T // PAGE
Q_TILES = NQ // P
LIST_ROWS = 16
SCALE_ROWS = 16
QUADRANT = 32
PARK_FIRST = 32
PARK_STEP = 4
PARKED = slice(PARK_FIRST, PARK_FIRST + SCALE_ROWS * PARK_STEP, PARK_STEP)
VS_ROW = 4

FLOPS = 2 * NQ * N * (D + DV)


def place_scale_rows(nc, plane, parked):
    for quad in range(P // QUADRANT):
        first = PARK_FIRST + quad * PACK * PARK_STEP
        nc.sync.dma_start(
            plane[quad * QUADRANT : quad * QUADRANT + PACK, :].bitcast(I32),
            parked[first : first + PACK * PARK_STEP : PARK_STEP, :].bitcast(I32),
        )


def tile_attend_pkv8_relu2_kernel(tc, qT, k_words, k_scales, v_words, v_scales, vs, offs, voffs, out):
    nc = tc.nc
    with ExitStack() as ctx:
        lists = ctx.enter_context(tc.tile_pool(name="lists", bufs=1))
        sb = ctx.enter_context(tc.tile_pool(name="sb", bufs=1))
        psum = ctx.enter_context(tc.psum_pool(name="psum", bufs=1))

        k_list = lists.tile([P, N // LIST_ROWS], U16, name="k_list")
        v_list = lists.tile([P, PAGES * DV // LIST_ROWS], U16, name="v_list")
        q_raw = sb.tile([P, PACK, NQ], F32, name="q_raw", align_bytes=64)
        vsc_pool = sb.tile([P, POOL_PAGES * DV], U8, name="vsc_pool")
        ks_pool = sb.tile([P, T], U8, name="ks_pool", tag="ks_then_v", align_bytes=64)
        k_pool = sb.tile([P, T], U32, name="k_pool")
        ts_pool = sb.tile([P, T], F32, name="ts_pool", tag="ts_then_vsc")
        ks_plane = sb.tile([P, N], U8, name="ks_plane", align_bytes=64)
        ident = sb.tile([P, P], F32, name="ident")

        vsc_plane = sb.tile([P, PAGES * DV], U8, name="vsc_plane", align_bytes=64)
        nc.vector.memset(ks_pool[:].bitcast(I32), 0)
        nc.vector.memset(ts_pool[:], 0.0)
        nc.vector.memset(vsc_pool[:].bitcast(I32), 0)
        nc.vector.memset(ident[:], 0.0)
        make_identity(nc, ident[:], nomemset=True)

        k_dram = k_words[0].rearrange("p t r -> p (t r)").bitcast(I32)
        nc.sync.dma_start(k_list[:], offs)
        nc.sync.dma_start(v_list[:], voffs)
        nc.sync.dma_start(q_raw[:], qT[0].rearrange("(p j) c -> p j c", j=PACK))
        nc.sync.dma_start(ks_pool[PARKED, :].bitcast(I32), k_scales[0].bitcast(I32))
        nc.sync.dma_start(k_pool[:, : T // 2].bitcast(I32), k_dram[:, : T // 2])
        nc.sync.dma_start(ts_pool[VS_ROW : VS_ROW + 1, :], vs[0:1, :])
        nc.sync.dma_start(
            vsc_pool[PARKED, :].bitcast(I32).rearrange("f (u e) -> f u e", u=POOL_PAGES),
            v_scales.bitcast(I32).rearrange("u f e -> f u e"),
        )
        nc.sync.dma_start(k_pool[:, T // 2 :].bitcast(I32), k_dram[:, T // 2 :])

        ks_parked = sb.tile([P, N], U8, name="ks_parked")
        nc.vector.tensor_copy(ks_parked[:], ks_pool[:].indirect(k_list[:]))
        place_scale_rows(nc, ks_plane, ks_parked)

        v_pool = sb.tile([P, POOL_PAGES * DV], U32, name="v_pool", tag="ks_then_v", align_bytes=64)
        nc.sync.dma_start(
            v_pool[:].bitcast(I32).rearrange("p (u e) -> p u e", u=POOL_PAGES),
            v_words.rearrange("u p e r -> p u (e r)").bitcast(I32),
        )

        q_bf = sb.tile([P, NQ, PACK], BF16, name="q_bf", align_bytes=64)
        nc.scalar.activation(q_bf[:], q_raw[:].rearrange("p j c -> p c j"), ACT.Copy)
        q_codes = sb.tile([P, NQ], U32, name="q_codes", align_bytes=64)
        q_plane = sb.tile([P, NQ], U8, name="q_plane", align_bytes=64)
        nc.vector.quantize_mx(q_codes[:].bitcast(FP8X4), q_plane[:], q_bf[:].rearrange("p c j -> p (c j)"))


        cols = PAGE // LIST_ROWS
        ts_cols = [sb.tile([P, PACK], F32, name=f"ts_col{u}") for u in range(PAGES)]

        def gather_token_scales(u, ts_row):
            nc.vector.tensor_copy(ts_row[:], ts_pool[:].indirect(k_list[:, u * cols : (u + 1) * cols]))

        def turn_token_scales(u, ts_row, bank_tag, copy):
            bank = psum.tile([P, PACK, P], F32, name=f"ts_bank{u}", tag=bank_tag)
            for r in range(PACK):
                nc.tensor.transpose(bank[:, r, :], ts_row[:, r:PAGE:PACK], ident[:])
            copy(ts_cols[u][:], bank[:, :, VS_ROW])

        ts_row0 = sb.tile([P, PAGE], F32, name="ts_row0")
        gather_token_scales(0, ts_row0)
        turn_token_scales(0, ts_row0, "turn2", nc.scalar.copy)
        ts_row1 = sb.tile([P, PAGE], F32, name="ts_row1")
        gather_token_scales(1, ts_row1)
        turn_token_scales(1, ts_row1, "turn1", nc.scalar.copy)
        vsc_parked = sb.tile([P, PAGES * DV], U8, name="vsc_parked", tag="ts_then_vsc")
        nc.vector.tensor_copy(vsc_parked[:], vsc_pool[:].indirect(v_list[:]))
        place_scale_rows(nc, vsc_plane, vsc_parked)

        k_pages = []
        for u in range(PAGES):
            k_page = sb.tile([P, PAGE], U32, name=f"k_page{u}", align_bytes=64)
            nc.vector.tensor_copy(k_page[:], k_pool[:].indirect(k_list[:, u * cols : (u + 1) * cols]))
            k_pages.append(k_page)
        v_pages = sb.tile([P, PAGES * DV], U32, name="v_pages", align_bytes=64)
        nc.vector.tensor_copy(v_pages[:], v_pool[:].indirect(v_list[:]))

        part_sum = sb.tile([P, PAGES, Q_TILES], F32, name="part_sum")
        acc = [psum.tile([P, DV], F32, name=f"acc{h}") for h in range(Q_TILES)]
        for u in range(PAGES):
            w = sb.tile([P, Q_TILES, P, PACK], BF16, name=f"w{u}", align_bytes=64)
            w_codes = sb.tile([P, NQ], U32, name=f"w_codes{u}", align_bytes=64)
            w_plane = sb.tile([P, NQ], U8, name=f"w_plane{u}", align_bytes=64)
            joint = u in [0]
            for h in range(Q_TILES):
                rows = slice(h * P, (h + 1) * P)
                unit = u * Q_TILES + h
                score = psum.tile([P, PAGE], F32, name=f"score{unit}", tag=f"score{unit % 3}")
                nc.tensor.matmul_mx(
                    score[:],
                    lhsT=q_codes[:, rows].bitcast(FP8X4),
                    lhsT_scale=q_plane[:, rows],
                    rhs=k_pages[u][:].bitcast(FP8X4),
                    rhs_scale=ks_plane[:, u * PAGE : (u + 1) * PAGE],
                    start=True,
                    stop=True,
                )
                pos = sb.tile([P, PACK, P], F32, name=f"pos{unit}")
                if unit in [3]:
                    nc.vector.tensor_scalar(pos[:], score[:].rearrange("q (s r) -> q r s", r=PACK), 0.0, None, ALU.max)
                else:
                    nc.scalar.activation(pos[:], score[:].rearrange("q (s r) -> q r s", r=PACK), ACT.Relu)
                p = sb.tile([P, PACK, P], F32, name=f"p{unit}")
                nc.scalar.activation(p[:], pos[:], ACT.Square, accum_out=part_sum[:, u, h : h + 1])
                turned = psum.tile([P, PACK, P], F32, name=f"turned{unit}", tag=f"turn{unit % 3}")
                for r in range(PACK):
                    nc.tensor.transpose(turned[:, r, :], p[:, r, :], ident[:])
                nc.vector.tensor_tensor(
                    w[:, h, :, :],
                    turned[:].rearrange("s r q -> s q r"),
                    ts_cols[u][:].unsqueeze(1).to_broadcast([P, P, PACK]),
                    ALU.mult,
                )
                if not joint:
                    nc.vector.quantize_mx(w_codes[:, rows].bitcast(FP8X4), w_plane[:, rows], w[:, h, :, :].rearrange("s q r -> s (q r)"))
            if joint:
                nc.vector.quantize_mx(w_codes[:].bitcast(FP8X4), w_plane[:], w[:].rearrange("s h q r -> s (h q r)"))
            for h in range(Q_TILES):
                rows = slice(h * P, (h + 1) * P)
                nc.tensor.matmul_mx(
                    acc[h][:],
                    lhsT=w_codes[:, rows].bitcast(FP8X4),
                    lhsT_scale=w_plane[:, rows],
                    rhs=v_pages[:, u * DV : (u + 1) * DV].bitcast(FP8X4),
                    rhs_scale=vsc_plane[:, u * DV : (u + 1) * DV],
                    start=(u == 0),
                    stop=(u == PAGES - 1),
                )
        total = sb.tile([P, Q_TILES], F32, name="total")
        nc.vector.scalar_tensor_tensor(total[:], part_sum[:, 0, :], 1.0, part_sum[:, 1, :], ALU.add, ALU.add)
        inv = sb.tile([P, Q_TILES], F32, name="inv")
        nc.vector.reciprocal(inv[:], total[:])
        for h in range(Q_TILES):
            y = sb.tile([P, DV], F32, name=f"y{h}")
            nc.scalar.activation(y[:], acc[h][:], ACT.Copy, scale=inv[:, h : h + 1])
            nc.scalar.dma_start(out[0, h * P : (h + 1) * P, :], y[:])
